import numpy as np
import ml_dtypes

BF16 = ml_dtypes.bfloat16


def bf(x):
    return np.asarray(x, np.float32).astype(BF16)


def f32(x):
    return np.asarray(x, np.float32)


def f64(x):
    return np.asarray(x).astype(np.float64)


def striped(idx):
    return np.tile(idx.reshape(-1, 16).T, (8, 1))


A, S, K, M, N, E, Q = 256, 256, 256, 256, 192, 2, 96


def setup_inputs():
    return {"a": bf(np.random.standard_normal((A, S))), "wd": bf(np.random.standard_normal((A, M)) / np.sqrt(A)), "x": bf(np.random.standard_normal((K, N))), "w": bf(1.2 * np.random.standard_normal((E, K, M)) / np.sqrt(K)), "s": f32(0.5 + np.random.random_sample((M, 1))), "offs": striped(np.random.permutation(S)[:N])}


def reference(a, wd, x, w, s, offs):
    idx = offs[:16].T.reshape(-1)
    z = f64(wd).T @ f64(a)
    for e in range(E):
        z[:, idx[e * Q : (e + 1) * Q]] += f64(w)[e].T @ f64(x)[:, e * Q : (e + 1) * Q]
    z = z / np.sqrt((z**2).mean(axis=0, keepdims=True) + 1e-5) * f64(s)
    return z

@@ -1,0 +1,82 @@
+import concourse.mybir as mybir
+
+BF16, F32, U16 = mybir.dt.bfloat16, mybir.dt.float32, mybir.dt.uint16
+ACT = mybir.ActivationFunctionType
+MULT = mybir.AluOpType.mult
+
+P = 128
+D = 256
+K = 256
+M = 256
+S = 256
+N = 192
+E = 2
+PIECE = N // E
+LANES = 16
+EPS = 1e-5
+
+FLOPS = 2 * D * M * S + 2 * K * M * N + 2 * M * M * S // P + 6 * M * S
+
+
+def tile_rows_placenorm_proj_kernel(tc, a, wd, x, w, s, offs, out):
+    nc = tc.nc
+    d_blocks, k_blocks, m_blocks = D // P, K // P, M // P
+
+    with (
+        tc.tile_pool(name="held", bufs=1) as held,
+        tc.psum_pool(name="psum", bufs=1) as psum,
+    ):
+        a_t = held.tile([P, d_blocks, S], BF16, name="a_t")
+        wd_t = held.tile([P, d_blocks, M], BF16, name="wd_t")
+        offsets = held.tile([P, N // LANES], U16, name="offsets")
+        x_t = held.tile([P, k_blocks, N], BF16, name="x_t")
+        w_t = held.tile([P, E, k_blocks, M], BF16, name="w_t")
+        gain = held.tile([P, m_blocks], F32, name="gain")
+
+        nc.sync.dma_start(a_t[:], a.rearrange("(p b) i -> p b i", b=d_blocks))
+        nc.sync.dma_start(wd_t[:], wd.rearrange("(p b) m -> p b m", b=d_blocks))
+        nc.sync.dma_start(offsets[:], offs)
+        nc.sync.dma_start(x_t[:], x.rearrange("(p b) j -> p b j", b=k_blocks))
+        for e in range(E):
+            nc.sync.dma_start(w_t[:, e], w[e].rearrange("(p b) m -> p b m", b=k_blocks))
+        nc.sync.dma_start(gain[:], s.rearrange("(f p) o -> p (f o)", p=P))
+
+        ones = held.tile([P, P], BF16, name="ones")
+        nc.vector.memset(ones[:], 1.0)
+        eps = held.tile([P, 1], F32, name="eps")
+        nc.vector.memset(eps[:], EPS)
+        early = held.tile([P, 1], F32, name="early")
+        nc.scalar.activation(early[:], eps[:], ACT.Abs_reciprocal_sqrt, bias=eps[:])
+
+        z = [psum.tile([P, S], F32, name=f"z{f}") for f in range(m_blocks)]
+        for f in range(m_blocks):
+            for b in range(d_blocks):
+                nc.tensor.matmul(
+                    z[f][:], wd_t[:, b, f * P : (f + 1) * P], a_t[:, b, :], start=b == 0, stop=False
+                )
+
+        cols = PIECE // LANES
+        for f in range(m_blocks):
+            for e in range(E):
+                for b in range(k_blocks):
+                    nc.tensor.matmul(
+                        z[f][:].indirect(offsets[:, e * cols : (e + 1) * cols]),
+                        w_t[:, e, b, f * P : (f + 1) * P],
+                        x_t[:, b, e * PIECE : (e + 1) * PIECE],
+                        start=False,
+                        stop=e == E - 1 and b == k_blocks - 1,
+                    )
+
+        total = psum.tile([P, S], F32, name="total")
+        for f in range(m_blocks):
+            square = held.tile([P, S], BF16, name=f"square{f}")
+            nc.scalar.activation(square[:], z[f][:], ACT.Square)
+            nc.tensor.matmul(total[:], ones[:], square[:], start=f == 0, stop=f == m_blocks - 1)
+
+        rnorm = held.tile([P, S], F32, name="rnorm")
+        nc.scalar.activation(rnorm[:], total[:], ACT.Abs_reciprocal_sqrt, bias=eps[:], scale=1.0 / M)
+
+        for f in range(m_blocks):
+            y = held.tile([P, S], F32, name=f"y{f}")
+            nc.vector.scalar_tensor_tensor(y[:], z[f][:], gain[:, f : f + 1], rnorm[:], MULT, MULT)
+            nc.sync.dma_start(out[f * P : (f + 1) * P, :], y[:])

@@ -14,8 +14,9 @@ E = 2
 PIECE = N // E
 LANES = 16
 EPS = 1e-5
+WARM_UP = 4
 
-FLOPS = 2 * D * M * S + 2 * K * M * N + 2 * M * M * S // P + 6 * M * S
+FLOPS = 2 * D * M * S + 2 * K * M * N + 5 * M * S
 
 
 def tile_rows_placenorm_proj_kernel(tc, a, wd, x, w, s, offs, out):
@@ -48,6 +49,12 @@ def tile_rows_placenorm_proj_kernel(tc, a, wd, x, w, s, offs, out):
         early = held.tile([P, 1], F32, name="early")
         nc.scalar.activation(early[:], eps[:], ACT.Abs_reciprocal_sqrt, bias=eps[:])
 
+        zeros = held.tile([P, 512], BF16, name="zeros")
+        nc.vector.memset(zeros[:], 0.0)
+        spare = psum.tile([P, 512], F32, name="spare")
+        for turn in range(WARM_UP):
+            nc.tensor.matmul(spare[:], zeros[:, :P], zeros[:], start=True, stop=True)
+
         z = [psum.tile([P, S], F32, name=f"z{f}") for f in range(m_blocks)]
         for f in range(m_blocks):
             for b in range(d_blocks):
@@ -56,8 +63,8 @@ def tile_rows_placenorm_proj_kernel(tc, a, wd, x, w, s, offs, out):
                 )
 
         cols = PIECE // LANES
-        for f in range(m_blocks):
-            for e in range(E):
+        for e in range(E):
+            for f in range(m_blocks):
                 for b in range(k_blocks):
                     nc.tensor.matmul(
                         z[f][:].indirect(offsets[:, e * cols : (e + 1) * cols]),

@@ -14,6 +14,7 @@ E = 2
 PIECE = N // E
 LANES = 16
 EPS = 1e-5
+HALVES = 2
 WARM_UP = 4
 
 FLOPS = 2 * D * M * S + 2 * K * M * N + 5 * M * S
@@ -40,7 +41,7 @@ def tile_rows_placenorm_proj_kernel(tc, a, wd, x, w, s, offs, out):
         nc.sync.dma_start(x_t[:], x.rearrange("(p b) j -> p b j", b=k_blocks))
         for e in range(E):
             nc.sync.dma_start(w_t[:, e], w[e].rearrange("(p b) m -> p b m", b=k_blocks))
-        nc.sync.dma_start(gain[:], s.rearrange("(f p) o -> p (f o)", p=P))
+        nc.sync.dma_start(gain[:], s.rearrange("(p f) o -> p (f o)", f=m_blocks))
 
         ones = held.tile([P, P], BF16, name="ones")
         nc.vector.memset(ones[:], 1.0)
@@ -59,7 +60,7 @@ def tile_rows_placenorm_proj_kernel(tc, a, wd, x, w, s, offs, out):
         for f in range(m_blocks):
             for b in range(d_blocks):
                 nc.tensor.matmul(
-                    z[f][:], wd_t[:, b, f * P : (f + 1) * P], a_t[:, b, :], start=b == 0, stop=False
+                    z[f][:], wd_t[:, b, f::m_blocks], a_t[:, b, :], start=b == 0, stop=False
                 )
 
         cols = PIECE // LANES
@@ -68,22 +69,28 @@ def tile_rows_placenorm_proj_kernel(tc, a, wd, x, w, s, offs, out):
                 for b in range(k_blocks):
                     nc.tensor.matmul(
                         z[f][:].indirect(offsets[:, e * cols : (e + 1) * cols]),
-                        w_t[:, e, b, f * P : (f + 1) * P],
+                        w_t[:, e, b, f::m_blocks],
                         x_t[:, b, e * PIECE : (e + 1) * PIECE],
                         start=False,
                         stop=e == E - 1 and b == k_blocks - 1,
                     )
 
-        total = psum.tile([P, S], F32, name="total")
+        half = S // HALVES
+        total = [psum.tile([P, half], F32, name=f"total{h}") for h in range(HALVES)]
         for f in range(m_blocks):
-            square = held.tile([P, S], BF16, name=f"square{f}")
-            nc.scalar.activation(square[:], z[f][:], ACT.Square)
-            nc.tensor.matmul(total[:], ones[:], square[:], start=f == 0, stop=f == m_blocks - 1)
+            for h in range(HALVES):
+                square = held.tile([P, half], BF16, name=f"square{f}{h}")
+                nc.scalar.activation(square[:], z[f][:, h * half : (h + 1) * half], ACT.Square)
+                nc.tensor.matmul(total[h][:], ones[:], square[:], start=f == 0, stop=f == m_blocks - 1)
 
-        rnorm = held.tile([P, S], F32, name="rnorm")
-        nc.scalar.activation(rnorm[:], total[:], ACT.Abs_reciprocal_sqrt, bias=eps[:], scale=1.0 / M)
-
-        for f in range(m_blocks):
-            y = held.tile([P, S], F32, name=f"y{f}")
-            nc.vector.scalar_tensor_tensor(y[:], z[f][:], gain[:, f : f + 1], rnorm[:], MULT, MULT)
-            nc.sync.dma_start(out[f * P : (f + 1) * P, :], y[:])
+        out_rows = out.rearrange("(p f) i -> p f i", f=m_blocks)
+        for h in range(HALVES):
+            tokens = slice(h * half, (h + 1) * half)
+            rnorm = held.tile([P, half], F32, name=f"rnorm{h}")
+            nc.scalar.activation(rnorm[:], total[h][:], ACT.Abs_reciprocal_sqrt, bias=eps[:], scale=1.0 / M)
+            y = held.tile([P, m_blocks, half], F32, name=f"y{h}")
+            for f in range(m_blocks):
+                nc.vector.scalar_tensor_tensor(
+                    y[:, f, :], z[f][:, tokens], gain[:, f : f + 1], rnorm[:], MULT, MULT
+                )
+            nc.sync.dma_start(out_rows[:, :, tokens], y[:])

@@ -15,7 +15,7 @@ PIECE = N // E
 LANES = 16
 EPS = 1e-5
 HALVES = 2
-WARM_UP = 4
+WARM_UP = 7
 
 FLOPS = 2 * D * M * S + 2 * K * M * N + 5 * M * S
 
@@ -39,9 +39,14 @@ def tile_rows_placenorm_proj_kernel(tc, a, wd, x, w, s, offs, out):
         nc.sync.dma_start(wd_t[:], wd.rearrange("(p b) m -> p b m", b=d_blocks))
         nc.sync.dma_start(offsets[:], offs)
         nc.sync.dma_start(x_t[:], x.rearrange("(p b) j -> p b j", b=k_blocks))
-        for e in range(E):
-            nc.sync.dma_start(w_t[:, e], w[e].rearrange("(p b) m -> p b m", b=k_blocks))
+        nc.sync.dma_start(w_t[:], w.rearrange("e (p b) m -> p e b m", b=k_blocks))
         nc.sync.dma_start(gain[:], s.rearrange("(p f) o -> p (f o)", f=m_blocks))
+
+        zeros = held.tile([P, S], BF16, name="zeros")
+        nc.vector.memset(zeros[:], 0.0)
+        spare = psum.tile([P, S], F32, name="spare")
+        for turn in range(WARM_UP):
+            nc.tensor.matmul(spare[:], zeros[:, :P], zeros[:], start=True, stop=True)
 
         ones = held.tile([P, P], BF16, name="ones")
         nc.vector.memset(ones[:], 1.0)
@@ -49,12 +54,6 @@ def tile_rows_placenorm_proj_kernel(tc, a, wd, x, w, s, offs, out):
         nc.vector.memset(eps[:], EPS)
         early = held.tile([P, 1], F32, name="early")
         nc.scalar.activation(early[:], eps[:], ACT.Abs_reciprocal_sqrt, bias=eps[:])
-
-        zeros = held.tile([P, 512], BF16, name="zeros")
-        nc.vector.memset(zeros[:], 0.0)
-        spare = psum.tile([P, 512], F32, name="spare")
-        for turn in range(WARM_UP):
-            nc.tensor.matmul(spare[:], zeros[:, :P], zeros[:], start=True, stop=True)
 
         z = [psum.tile([P, S], F32, name=f"z{f}") for f in range(m_blocks)]
         for f in range(m_blocks):
@@ -64,8 +63,8 @@ def tile_rows_placenorm_proj_kernel(tc, a, wd, x, w, s, offs, out):
                 )
 
         cols = PIECE // LANES
-        for e in range(E):
-            for f in range(m_blocks):
+        for f in range(m_blocks):
+            for e in range(E):
                 for b in range(k_blocks):
                     nc.tensor.matmul(
                         z[f][:].indirect(offsets[:, e * cols : (e + 1) * cols]),

import concourse.mybir as mybir

BF16, F32, U16 = mybir.dt.bfloat16, mybir.dt.float32, mybir.dt.uint16
ACT = mybir.ActivationFunctionType
MULT = mybir.AluOpType.mult

P = 128
D = 256
K = 256
M = 256
S = 256
N = 192
E = 2
PIECE = N // E
LANES = 16
EPS = 1e-5
HALVES = 2
WARM_UP = 7

FLOPS = 2 * D * M * S + 2 * K * M * N + 5 * M * S


def tile_rows_placenorm_proj_kernel(tc, a, wd, x, w, s, offs, out):
    nc = tc.nc
    d_blocks, k_blocks, m_blocks = D // P, K // P, M // P

    with (
        tc.tile_pool(name="held", bufs=1) as held,
        tc.psum_pool(name="psum", bufs=1) as psum,
    ):
        a_t = held.tile([P, d_blocks, S], BF16, name="a_t")
        wd_t = held.tile([P, d_blocks, M], BF16, name="wd_t")
        offsets = held.tile([P, N // LANES], U16, name="offsets")
        x_t = held.tile([P, k_blocks, N], BF16, name="x_t")
        w_t = held.tile([P, E, k_blocks, M], BF16, name="w_t")
        gain = held.tile([P, m_blocks], F32, name="gain")

        nc.sync.dma_start(a_t[:], a.rearrange("(p b) i -> p b i", b=d_blocks))
        nc.sync.dma_start(wd_t[:], wd.rearrange("(p b) m -> p b m", b=d_blocks))
        nc.sync.dma_start(offsets[:], offs)
        nc.sync.dma_start(x_t[:], x.rearrange("(p b) j -> p b j", b=k_blocks))
        nc.sync.dma_start(w_t[:], w.rearrange("e (p b) m -> p e b m", b=k_blocks))
        nc.sync.dma_start(gain[:], s.rearrange("(p f) o -> p (f o)", f=m_blocks))

        zeros = held.tile([P, S], BF16, name="zeros")
        nc.vector.memset(zeros[:], 0.0)
        spare = psum.tile([P, S], F32, name="spare")
        for turn in range(WARM_UP):
            nc.tensor.matmul(spare[:], zeros[:, :P], zeros[:], start=True, stop=True)

        ones = held.tile([P, P], BF16, name="ones")
        nc.vector.memset(ones[:], 1.0)
        eps = held.tile([P, 1], F32, name="eps")
        nc.vector.memset(eps[:], EPS)
        early = held.tile([P, 1], F32, name="early")
        nc.scalar.activation(early[:], eps[:], ACT.Abs_reciprocal_sqrt, bias=eps[:])

        z = [psum.tile([P, S], F32, name=f"z{f}") for f in range(m_blocks)]
        for f in range(m_blocks):
            for b in range(d_blocks):
                nc.tensor.matmul(
                    z[f][:], wd_t[:, b, f::m_blocks], a_t[:, b, :], start=b == 0, stop=False
                )

        cols = PIECE // LANES
        for f in range(m_blocks):
            for e in range(E):
                for b in range(k_blocks):
                    nc.tensor.matmul(
                        z[f][:].indirect(offsets[:, e * cols : (e + 1) * cols]),
                        w_t[:, e, b, f::m_blocks],
                        x_t[:, b, e * PIECE : (e + 1) * PIECE],
                        start=False,
                        stop=e == E - 1 and b == k_blocks - 1,
                    )

        half = S // HALVES
        total = [psum.tile([P, half], F32, name=f"total{h}") for h in range(HALVES)]
        for f in range(m_blocks):
            for h in range(HALVES):
                square = held.tile([P, half], BF16, name=f"square{f}{h}")
                nc.scalar.activation(square[:], z[f][:, h * half : (h + 1) * half], ACT.Square)
                nc.tensor.matmul(total[h][:], ones[:], square[:], start=f == 0, stop=f == m_blocks - 1)

        out_rows = out.rearrange("(p f) i -> p f i", f=m_blocks)
        for h in range(HALVES):
            tokens = slice(h * half, (h + 1) * half)
            rnorm = held.tile([P, half], F32, name=f"rnorm{h}")
            nc.scalar.activation(rnorm[:], total[h][:], ACT.Abs_reciprocal_sqrt, bias=eps[:], scale=1.0 / M)
            y = held.tile([P, m_blocks, half], F32, name=f"y{h}")
            for f in range(m_blocks):
                nc.vector.scalar_tensor_tensor(
                    y[:, f, :], z[f][:, tokens], gain[:, f : f + 1], rnorm[:], MULT, MULT
                )
            nc.sync.dma_start(out_rows[:, :, tokens], y[:])
